import numpy as np, ml_dtypes
CORES = [3,11,19,27,35,43,51,59]
N = 8
BF = ml_dtypes.bfloat16
def gentries(a):
    return np.ascontiguousarray(a.reshape(8, 16, -1).transpose(0, 2, 1)).reshape(8, -1)
def gtable(e):
    e = np.asarray(e); return np.ascontiguousarray(e.reshape(8, -1, 16).transpose(0, 2, 1)).reshape(128, -1).astype(np.int32)
V, CAP, RO, DEC = 256, 32, 3, 24
S = N * V; E = 16 * S; D = 16 * N
def level(rng, *shape):
    return (256 * rng.random(shape[:2] + (1,) + shape[3:]) * rng.random(shape)).astype(np.int64)
def parts(rng):
    fan = np.argsort(rng.random((N, 8, E)), axis=-1)
    lo = rng.choice(np.array([0, 32, 96]), (N, 8, 1)); cost = lo + ((256 - lo) * rng.random((N, 8, E))).astype(np.int64)
    th = np.stack([rng.permutation(np.array([120, 250, 500, 900, 1300, 1600, 1800, 2000])) for q in range(N)]) + rng.integers(0, 40, (N, 8))
    x = level(rng, N, 8, 16, V); dv = np.where(rng.random((N, 8, 1, RO, V)) < 0.15, level(rng, N, 8, 16, RO, V), 0)
    return x, fan, cost, th, dv
def pack(x, fan, cost, th, dv):
    return {"x0": np.ascontiguousarray(x.reshape(N, 128, V)).astype(np.int32), "fan": np.stack([gtable(a) for a in fan]), "cost": np.ascontiguousarray(cost).astype(np.int32),
            "th": np.ascontiguousarray(np.repeat(th, 16, axis=1)[:, :, None]).astype(np.int32), "drv": np.ascontiguousarray(dv.reshape(N, 128, RO * V)).astype(np.int32)}
def setup_inputs(rng):
    return pack(*parts(rng))
def setup_inputs_room(rng):
    x, fan, cost, th, dv = parts(rng); th = rng.integers(200, 1501, (N, 8)); dv[:, :, :, 0] = 0
    for q in range(N):
        for g in range(8):
            o = rng.permutation(V); t = int(th[q, g]); n = int(rng.choice(np.array([0, 1, CAP - 1, CAP, CAP + 1, V])))
            if q == 0: n = (CAP, CAP + 1, V, CAP - 1, 1, 0, CAP, CAP + 1)[g]
            x[q, g][:, o[:n]] = DEC + (t + 15) // 16 + rng.integers(0, 100, (16, n))
            x[q, g][:, o[n:]] = rng.integers(0, DEC + (t - 1) // 16 + 1, (16, V - n))
    return pack(x, fan, cost, th, dv)
def setup_inputs_ties(rng):
    x, fan, cost, th, dv = parts(rng); th = rng.choice(np.array([1, 2, 15, 16, 17, 255, 1000, 3000]), (N, 8))
    share = np.where(np.arange(8) % 2 == 0, 0.7, 0.1)[None, :, None, None]
    goal = th[:, :, None, None] - 1 + np.where(rng.random((N, 8, 1, V)) < share, rng.integers(1, 3, (N, 8, 1, V)), 0)
    m = goal // 16; y = m + (np.arange(16)[:, None] < goal % 16)
    d = ((np.minimum(m, 254 - DEC - m) + 1) * rng.random((N, 8, 8, V))).astype(np.int64)
    y[:, :, :8] += d; y[:, :, 8:] -= d
    x = np.where(y > 0, y + DEC, rng.integers(0, DEC + 1, y.shape)); dv[:, :, :, 0] = 0
    th[:, 0] = 16 * DEC; th[:, 1] = 16 * DEC + 1
    x[:, :2] = rng.integers(RO * DEC + 1, 256, (N, 2, 16, V)); cost[:, :2] = 255; dv[:, :2] = 0
    x[:, 7] = 0; dv[:, 7] = 0; cost[:, 7] = rng.integers(254, 256, (N, E))
    for q in range(N):
        t = (4080, 4079, 4077, 2049)[q % 4]; th[q, 7] = t; o = rng.permutation(V)[:CAP]
        w = np.repeat(np.array([t - 1, t, 4080]), [CAP // 2, CAP // 4, CAP - CAP // 2 - CAP // 4])
        dv[q, 7][:, 0][:, o] = w // 16 + (np.arange(16)[:, None] < w % 16)
    return pack(x, fan, cost, th, dv)
def setup_inputs_alike(rng):
    x, fan, cost, th, dv = parts(rng); ar = np.arange(E); s = ar // 16; i = ar % 16
    fan[:, 0] = ar; fan[:, 1] = ar[::-1]; fan[:, 2] = (16 * (s // V) + i) * V + s % V
    for q in range(N): fan[q, 3] = (16 * rng.permutation(S)[:, None] + np.arange(16)).reshape(-1)
    fan[:, 5] = fan[0, 5].copy()
    cost[:, ::2] = rng.choice(np.array([0, 1, 254, 255]), (N, 4, E))
    c = cost[:, 2].reshape(N, D, V).copy(); h = c[:, :, ::2].shape[2]
    c[:, :D - 4, ::2] = rng.integers(254, 256, (N, D - 4, h)); c[:, D - 4:, ::2] = rng.integers(0, 2, (N, 4, h))
    cost[:, 2] = c.reshape(N, E); dv[:, 2, :, :, 0] = 0
    x = rng.choice(np.array([0, DEC - 1, DEC, DEC + 1, 128, 255]), (N, 8, 16, V)); x[..., 0] = 255; x[..., V - 1] = 255
    th = rng.choice(np.array([1, 16, 300, 600]), (N, 8)); th[:, 0] = 1; th[N - 1, 7] = 600
    return pack(x, fan, cost, th, dv)
def setup_inputs_quiet(rng):
    x, fan, cost, th, dv = parts(rng); x = np.minimum(x, 254); dv = np.minimum(dv, 254); h = rng.permutation(8); q = rng.permutation(N)
    th[q[0]] = 1; th[:, h[1]] = 1; th[q[1]] = 4080; th[q[1], h[2]] = 1; th[:, h[0]] = 4080
    x[:, h[1]] = 0; dv[:, h[1]] = 0; dv[q[0], h[1], :, 0, V - 1] = 254
    a = int(h[3]); x[:, a] = 0; dv[:, a, :, :2] = 0
    dv[:, a, :, 2] = np.where(rng.random((N, 1, V)) < 0.3, rng.integers(130, 255, (N, 16, V)), 0)
    b = int(h[4]); x[:, b] = 0; dv[:, b] = 0; cost[:, b] = rng.integers(200, 256, (N, E))
    th[:, b] = rng.integers(1000, 1601, N); th[q[1], b] = 4080; k = max(RO - 4, 0)
    for r in range(N):
        n = int(rng.integers(CAP // 2, CAP + 1)); o = rng.permutation(V)[:n]
        dv[r, b][:, k][:, o] = rng.integers(100, 121, (16, n)); dv[r, b][:, k + 1][:, o] = rng.integers(230, 255, (16, n))
    return pack(x, fan, cost, th, dv)
def setup_inputs_spread(rng):
    x, fan, cost, th, dv = parts(rng)
    x = np.minimum((np.exp2(8 * rng.random((N, 8, 1, V))) * rng.random((N, 8, 16, V))).astype(np.int64), 255)
    w = np.exp2(8 * rng.random((N, 8, E))); cost = np.minimum(np.where(rng.random((N, 8, E)) < 0.5, w - 1, 256 - w).astype(np.int64), 255)
    th = np.minimum(np.maximum(np.exp2(12 * rng.random((N, 8))).astype(np.int64), 1), 4080)
    v = np.minimum((np.exp2(8 * rng.random((N, 8, 1, RO, V))) * rng.random((N, 8, 16, RO, V))).astype(np.int64), 255)
    dv = np.where(rng.random((N, 8, 1, RO, V)) < 0.5 * rng.random((N, 8, 1, RO, 1)), v, 0)
    return pack(x, fan, cost, th, dv)
def check_inputs(d):
    bad = []
    for k, lo, hi in (("x0", 0, 255), ("fan", 0, E - 1), ("cost", 0, 255), ("th", 1, 4080), ("drv", 0, 255)):
        if np.min(d[k]) < lo or np.max(d[k]) > hi: bad.append("range of " + k)
    if not all(np.array_equal(np.sort(gentries(a), axis=1), np.tile(np.arange(E), (8, 1))) for a in d["fan"]): bad.append("every slot once in fan")
    t = d["th"].reshape(-1, 16)
    if np.any(t != t[:, :1]): bad.append("th alike in a group")
    return bad
def reference(x0, fan, cost, th, drv):
    x = x0.astype(np.int64).reshape(N, 8, 16, V); t = th.astype(np.int64).reshape(N, 8, 16)[:, :, :1]; dv = drv.astype(np.int64).reshape(N, 8, 16, RO, V)
    c = cost.astype(np.int16).reshape(N, 8, 1, D, V)
    fl = np.stack([gentries(a) for a in fan]).astype(np.int64).reshape(N, 8, S, 16)
    slots = np.zeros((N, 8, 16, E), np.int16); last = np.zeros((N, 8, 16, V), np.int64)
    for k in range(RO):
        best = np.stack([np.max(slots[r].reshape(8, 16, D, V) - c[r], axis=2) for r in range(N)]).astype(np.int64)
        x = np.maximum(np.maximum(x - DEC, dv[:, :, :, k]), np.maximum(best, 0))
        changed = np.add.reduce(np.abs(x - last), axis=2) >= t
        h = changed.astype(np.int64); sent = changed & (np.add.accumulate(h, axis=2) - h < CAP)
        last = np.where(sent[:, :, None, :], x, last)
        for g in range(8):
            s = np.flatnonzero(sent[:, g].reshape(-1))
            col = x[:, g].transpose(1, 0, 2).reshape(16, S)[:, s].astype(np.int16)
            for r in range(N):
                slots[r, g][:, fl[r, g][s]] = col[:, :, None]
    return {"yx": x.reshape(N, 128, V).astype(np.float32), "yl": last.reshape(N, 128, V).astype(np.float32)}

@@ -1,0 +1,272 @@
+from concourse.bass import DstId, RemoteDMATransfer
+from concourse.mybir import AluOpType as A, AxisListType, ActivationFunctionType as F
+
+N, V, CAP, RO, DEC = 8, 256, 32, 3, 24
+P = 128
+W = V * P
+Z = -255.0
+U = W // 16
+NO = (N - 1) * CAP
+HV = V // 2
+L = V + CAP
+X, K, C, Q, B = 16511.5, 128.0 / 32769.0, 12582912.0, 32769.0, 16383.248046875
+
+SCRATCH = {
+    "x0i": ("sbuf", [128, V], "int32"), "dri": ("sbuf", [128, RO * V], "int32"), "thi": ("sbuf", [128, 1], "int32"),
+    "thf": ("sbuf", [128, 1], "float32"), "th0": ("sbuf", [128, 1], "float32"), "drs": ("sbuf", [128, RO * V], "bfloat16"),
+    "fani": ("sbuf", [128, 2048], "int32"), "ci": ("sbuf", [128, 8, V], "int32"),
+    "rc": ("sbuf", [128, V, 9], "bfloat16"),
+    "sel": ("sbuf", [128, 2048], "bfloat16"), "ones": ("sbuf", [128, 512], "bfloat16"), "nones": ("sbuf", [128, 128], "bfloat16"),
+    "ns": ("sbuf", [128, 128], "bfloat16"), "bt": ("sbuf", [128, 128], "bfloat16"),
+    "b1": ("sbuf", [128, 128], "bfloat16"), "b2": ("sbuf", [128, 128], "bfloat16"), "bm": ("sbuf", [128, 128], "bfloat16"),
+    "d0": ("sbuf", [128, W], "bfloat16"), "d1": ("sbuf", [128, W], "bfloat16"), "so": ("sbuf", [128, HV * P], "bfloat16"),
+    "pi": ("sbuf", [128, 2], "int32"), "jc": ("sbuf", [128, 1], "float32"), "jb": ("sbuf", [128, 1], "float32"),
+    "c33": ("sbuf", [128, L], "bfloat16"), "xe": ("sbuf", [128, L], "bfloat16"), "la": ("sbuf", [128, L], "bfloat16"),
+    "a0": ("sbuf", [128, V], "bfloat16"), "mx": ("sbuf", [128, V], "bfloat16"),
+    "chg": ("sbuf", [128, L], "bfloat16"), "cum": ("sbuf", [128, L], "bfloat16"), "le": ("sbuf", [128, L], "bfloat16"),
+    "sg": ("sbuf", [128, L], "bfloat16"), "acc": ("sbuf", [128, 1], "float32"), "cnt": ("sbuf", [128, 2], "float32"),
+    "tt2": ("sbuf", [128, 2], "float32"), "raw": ("sbuf", [128, 2], "uint16"),
+    "sb0": ("sbuf", [128, CAP + 2], "bfloat16"), "sb1": ("sbuf", [128, CAP + 2], "bfloat16"),
+    "land0": ("sbuf", [128, N - 1, CAP + 2], "bfloat16"), "land1": ("sbuf", [128, N - 1, CAP + 2], "bfloat16"),
+    "base": ("sbuf", [128, N - 1, 2], "float32"), "idf": ("sbuf", [128, N - 1, 2], "float32"),
+    "ids": ("sbuf", [128, 2 * (N - 1)], "uint16"), "ido": ("sbuf", [128, 2], "uint16"),
+    "w": ("sbuf", [128, NO], "float32"), "h": ("sbuf", [128, NO], "float32"), "d": ("sbuf", [128, NO], "float32"),
+    "of": ("sbuf", [128, NO], "uint16"), "ex": ("sbuf", [128, NO * 16], "bfloat16"),
+    "wo": ("sbuf", [128, CAP], "float32"), "ho": ("sbuf", [128, CAP], "float32"), "dd": ("sbuf", [128, CAP], "float32"),
+    "ofo": ("sbuf", [128, CAP], "uint16"), "exo": ("sbuf", [128, CAP * 16], "bfloat16"),
+    "l32": ("sbuf", [128, L], "float32"), "x32": ("sbuf", [128, V], "float32"), "v32": ("sbuf", [128, CAP], "float32"),
+    "pd0": ("psum", [128, 1024], "float32"), "pd1": ("psum", [128, 1024], "float32"), "pd2": ("psum", [128, 1024], "float32"),
+    "ps": ("psum", [128, 512], "float32"), "pt": ("psum", [128, 512], "float32"),
+}
+DMAS = ["dx", "dd0", "dth", "dcost", "dfan", "dd1", "dz0", "dz1", "dyx", "dyl"]
+SEMAPHORES = ["v", "a", "p", "q", "arr0", "arr1", "sent0", "sent1"] + DMAS
+
+
+def rank_program(g, core, T, topo):
+    r = T.rank_of(core)
+    if r is None:
+        return
+    eng = {"v": g.vector, "a": g.scalar, "p": g.tensor, "q": g, "s": g.sync}
+    cnt, lw, lr, seen = {}, {}, {}, {e: {} for e in eng}
+
+    def need(e, deps):
+        for s in sorted(deps):
+            if seen[e].get(s, 0) < deps[s]:
+                eng[e].wait_ge(T.sem[s], deps[s])
+                seen[e][s] = deps[s]
+
+    def op(e, fn, rd, wr, sem=None, inc=1):
+        deps = {}
+        own = e if sem is None else None
+        for k in rd:
+            if k in lw:
+                s, c = lw[k]
+                deps[s] = max(deps.get(s, 0), c)
+        for k in wr:
+            if k in lw and not (e == "p" and lw[k][0] == "p"):
+                s, c = lw[k]
+                deps[s] = max(deps.get(s, 0), c)
+            for s, c in lr.get(k, {}).items():
+                if s != own:
+                    deps[s] = max(deps.get(s, 0), c)
+        need(e, deps)
+        ins = fn()
+        s = sem or e
+        cnt[s] = cnt.get(s, 0) + inc
+        ins.then_inc(T.sem[s], inc)
+        for k in rd:
+            lr.setdefault(k, {})[s] = cnt[s]
+        for k in wr:
+            lw[k] = (s, cnt[s])
+            lr[k] = {}
+
+    v, a, t = g.vector, g.scalar, g.tensor
+    zk = ["z%d" % u for u in range(16)]
+
+    def zu(u, n=1):
+        return T.d1[:, u * U:(u + n) * U]
+
+    def dma(e, out, in_, rd, wr, sem):
+        op(e, lambda: eng[e].dma_start(out, in_), rd, wr, sem, 16)
+
+    dma("s", T.x0i[:], T.x0[:], [], ["x0i"], "dx")
+    dma("s", T.dri[:, 0:V], T.drv[:, 0:V], [], ["dri0"], "dd0")
+    dma("s", T.thi[:], T.th[:], [], ["thi"], "dth")
+    for q in range(8):
+        dma("s", T.ci[:, q, :], T.cost[:, 16 * V * q:16 * V * (q + 1)], [], ["ci"], "dcost")
+    dma("s", T.fani[:], T.fan[:], [], ["fan"], "dfan")
+    dma("s", T.dri[:, V:3 * V], T.drv[:, V:3 * V], [], ["dri1"], "dd1")
+
+    op("v", lambda: v.memset(T.ones[:], 1.0), [], ["ones"])
+    op("v", lambda: v.memset(T.nones[:], -1.0), [], ["nones"])
+    op("q", lambda: g.affine_select(T.bt[:], T.ones[:, 0:128], [[-16, 8], [0, 16]], A.is_ge, 0.0, 0, 1), ["ones"], ["bt"])
+    op("q", lambda: g.affine_select(T.b1[:], T.bt[:], [[16, 8], [0, 16]], A.is_ge, 0.0, 15, -1), ["bt"], ["b1"])
+    op("q", lambda: g.iota(T.pi[:, 0:1], [[0, 1]], 0, 1), [], ["pi0"])
+
+    def select(k):
+        op("q", lambda: g.affine_select(T.sel[:, 512 * k:512 * k + 512], T.ones[:], [[-1, 4], [-16, 8], [0, 16]], A.is_equal, 0.0, -4 * k, 1),
+           ["ones"], ["sel%d" % k])
+        m = 3 if k == 3 else 4
+        s = T.sel[:, 512 * k:512 * k + 128 * m]
+        op("q", lambda: g.affine_select(s, s, [[-1, m], [-16, 8], [0, 16]], A.not_equal, -1.0, -4 * k - 1, 1), ["sel%d" % k], ["sel%d" % k])
+
+    op("q", lambda: g.affine_select(T.ns[:], T.nones[:], [[-16, 8], [0, 16]], A.is_equal, 0.0, 0, 1), ["nones"], ["ns"])
+    select(3)
+    op("v", lambda: v.memset(zu(0), Z), [], ["z0"])
+    op("v", lambda: v.memset(T.rc[:, :, 0], 1024.0), [], ["rc0"])
+    op("v", lambda: v.memset(T.c33[:], float(CAP + 1)), [], ["c33"])
+    op("v", lambda: v.memset(T.xe[:, V:L], Z), [], ["xp"])
+    op("v", lambda: v.memset(T.la[:], Z), [], ["la"])
+    op("v", lambda: v.tensor_scalar(T.pi[:, 1:2], T.pi[:, 0:1], 15, None, A.bitwise_and), ["pi0"], ["pi1"])
+    op("v", lambda: v.tensor_scalar(T.jc[:], T.pi[:, 1:2], 16.0, None, A.add), ["pi1"], ["jc"])
+    op("v", lambda: v.tensor_scalar(T.jb[:], T.pi[:, 1:2], 0.5, None, A.add), ["pi1"], ["jb"])
+    op("v", lambda: v.memset(zu(1, 2), Z), [], ["z1", "z2"])
+    for u in (3, 4):
+        op("a", lambda: a.activation(zu(u), zu(0), F.Copy), ["z0"], ["z%d" % u])
+    dma("s", zu(7, 3), zu(0, 3), ["z0", "z1", "z2"], ["z7", "z8", "z9"], "dz0")
+
+    def choose(k, last):
+        th = T.th0 if k == 0 else T.thf
+        op("v", lambda: v.tensor_scalar(T.chg[:, 0:V], T.ps[:, 0:V], th[:, 0:1], None, A.is_ge), ["ps", "thf", "th0"], ["chg"])
+        op("v", lambda: v.tensor_scalar(T.chg[:, V:L], T.ps[:, 0:CAP], th[:, 0:1], None, A.is_lt), ["ps", "thf", "th0"], ["chp"])
+        op("v", lambda: v.tensor_tensor_scan(T.cum[:], T.chg[:], T.c33[:], 0.0, A.add, A.min), ["chg", "chp", "c33"], ["cum"])
+        op("a", lambda: a.activation(T.sg[:], T.cum[:], F.Sign, bias=T.jb[:, 0:1], scale=-1.0, accum_out=T.acc[:]), ["cum", "jb"], ["sg", "acc"])
+        op("v", lambda: v.tensor_scalar(T.le[:], T.cum[:], T.jc[:, 0:1], None, A.is_le), ["cum", "jc"], ["le"])
+        op("v", lambda: v.tensor_reduce(T.cnt[:, 1:2], T.le[:], AxisListType.X, A.add), ["le"], ["cnt1"])
+        op("v", lambda: v.tensor_scalar(T.cnt[:, 0:1], T.acc[:], 0.5, L / 2.0, A.mult, A.add), ["acc"], ["cnt0"])
+        op("v", lambda: v.tensor_copy(T.raw[:], T.cnt[:]), ["cnt0", "cnt1"], ["raw"])
+        if last:
+            op("v", lambda: v.tensor_scalar(T.v32[:], T.xe[:, 0:L].indirect(T.raw[:, 0:2]), -Z, None, A.add), ["x", "xp", "raw"], ["v32"])
+            return
+        sb = T["sb%d" % k]
+        op("v", lambda: v.tensor_scalar(T.tt2[:], T.cnt[:], float(V), -float(V), A.is_ge, A.mult), ["cnt0", "cnt1"], ["tt2"])
+        op("v", lambda: v.tensor_copy(sb[:, 0:CAP], T.xe[:, 0:L].indirect(T.raw[:, 0:2])), ["x", "xp", "raw"], ["sbv%d" % k])
+        op("v", lambda: v.tensor_tensor(sb[:, CAP:CAP + 2], T.cnt[:], T.tt2[:], A.add), ["cnt0", "cnt1", "tt2"], ["sbi%d" % k])
+
+    def send(k):
+        sb = T["sb%d" % k]
+        need("q", {"v": max(lw["sbv%d" % k][1], lw["sbi%d" % k][1])})
+        ids, dsts = [], []
+        for s in range(1, N):
+            q = (r + s) % N
+            rid, pid, _ = topo.addr(T.cores[q])
+            ids.append(DstId(rid=rid, pnc=pid))
+            dsts.append(T["land%d" % k][:, r if r < q else r - 1, :])
+        peer = T.cores[(r + 1) % N]
+        g.remote_dma_fused([RemoteDMATransfer(dst_ids=ids, dma_engine_mask=topo.mask(core, peer), remote_sem=T.sem["arr%d" % k], srcs=[sb[:]], dsts=dsts)],
+                           local_sem=T.sem["sent%d" % k])
+        cnt["sent%d" % k] = len(topo.engines(core, peer))
+        n = 0
+        for q in range(N):
+            if q != r:
+                n += len(topo.engines(T.cores[q], core))
+        cnt["arr%d" % k] = n
+        lw["land%d" % k] = ("arr%d" % k, n)
+
+    def columns(idk, idap, w, h, d, of, tag):
+        op("v", lambda: v.tensor_scalar(w[:], T.fani[:, 0:2048].indirect(idap), X, K, A.subtract, A.mult), ["fan", idk], ["w" + tag])
+        op("v", lambda: v.tensor_scalar(h[:], w[:], C, C, A.add, A.subtract), ["w" + tag], ["h" + tag])
+        op("v", lambda: v.tensor_tensor(d[:], w[:], h[:], A.subtract), ["w" + tag, "h" + tag], ["d" + tag])
+        op("v", lambda: v.tensor_scalar(of[:], d[:], Q, B, A.mult, A.add), ["d" + tag], ["of" + tag])
+
+    def own(k):
+        sb = T["sb%d" % k]
+        op("v", lambda: v.tensor_scalar(T.ido[:], sb[:, CAP:CAP + 2], float(V * r), None, A.add), ["sbi%d" % k], ["ido"])
+        for i in range(16):
+            op("v", lambda: v.tensor_copy(T.exo[:, i::16], sb[:, 0:CAP]), ["sbv%d" % k], ["exo%d" % i])
+        columns("ido", T.ido[:, 0:2], T.wo, T.ho, T.dd, T.ofo, "o")
+        op("v", lambda: v.tensor_copy(T.d1[:, 0:W].indirect(T.ofo[:, 0:CAP]), T.exo[:]), ["ofo"] + ["exo%d" % i for i in range(16)], zk)
+
+    def others(k):
+        ld, lk = T["land%d" % k], "land%d" % k
+        ex = ["ex%d" % i for i in range(16)]
+        if k == 1:
+            for i in range(16):
+                op("a", lambda: a.activation(T.ex[:, i::16], ld[:, :, 0:CAP], F.Copy), [lk], [ex[i]])
+        op("v", lambda: v.tensor_tensor(T.idf[:], ld[:, :, CAP:CAP + 2], T.base[:], A.add), [lk, "base0", "base1"], ["idf"])
+        op("v", lambda: v.tensor_copy(T.ids[:], T.idf[:]), ["idf"], ["ids"])
+        columns("ids", T.ids[:, 0:2 * (N - 1)], T.w, T.h, T.d, T.of, "n")
+        if k == 0:
+            for i in range(16):
+                op("v", lambda: v.tensor_copy(T.ex[:, i::16], ld[:, :, 0:CAP]), [lk], [ex[i]])
+        op("v", lambda: v.tensor_copy(T.d1[:, 0:W].indirect(T.of[:, 0:NO]), T.ex[:]), ["ofn"] + ex, zk)
+
+    def scan():
+        for c in range(2):
+            lo, hi = c * HV, c * HV + HV
+            op("v", lambda: v.tensor_tensor_scan(T.so[:], T.d0[:, lo * P:hi * P], T.d1[:, lo * P:hi * P], 0.0, A.add, A.max),
+               zk + ["d0_%d_%d" % (c, j) for j in range(16)], ["so"])
+            op("v", lambda: v.tensor_tensor(T.a0[:, lo:hi], T.so[:, P - 1::P], T.pt[:, lo:hi], A.add), ["so", "pt"], ["a0_%d" % c])
+            op("v", lambda: v.tensor_tensor(T.xe[:, lo:hi], T.a0[:, lo:hi], T.pt[:, V + lo:V + hi], A.max), ["a0_%d" % c, "mm"], ["x"])
+        op("v", lambda: v.tensor_tensor(T.mx[:], T.xe[:, 0:V], T.la[:, 0:V], A.max), ["x", "la"], ["mx"])
+        op("p", lambda: t.matmul(T.ps[:, 0:V], T.bm[:], T.la[:, 0:V], True, False), ["bm", "la"], ["ps"])
+        op("p", lambda: t.matmul(T.ps[:, 0:V], T.bm[:], T.xe[:, 0:V], False, False), ["bm", "x"], ["ps"])
+        op("p", lambda: t.matmul(T.ps[:, 0:V], T.b2[:], T.mx[:], False, True), ["b2", "mx"], ["ps"])
+
+    def after(k):
+        op("v", lambda: v.tensor_copy(T.la[:, 0:L].indirect(T.raw[:, 0:2]), T["sb%d" % k][:, 0:CAP]), ["raw", "sbv%d" % k], ["la"])
+        op("v", lambda: v.tensor_scalar(T.a0[:], T.xe[:, 0:V], float(DEC), None, A.subtract), ["x"], ["a0_0", "a0_1"])
+        op("v", lambda: v.tensor_tensor(T.pt[:, V:2 * V], T.a0[:], T.drs[:, (k + 1) * V:(k + 2) * V], A.max), ["a0_0", "a0_1", "drs1", "pt"], ["mm"])
+        op("v", lambda: v.tensor_copy(T.xe[:, V:L], T.la[:, 0:CAP]), ["la"], ["xp"])
+
+    op("v", lambda: v.tensor_scalar(T.a0[:], T.x0i[:], DEC - Z, None, A.subtract), ["x0i"], ["a0_0", "a0_1"])
+    op("v", lambda: v.tensor_scalar(T.drs[:, 0:V], T.dri[:, 0:V], Z, None, A.add), ["dri0"], ["drs0"])
+    op("v", lambda: v.tensor_tensor(T.xe[:, 0:V], T.a0[:], T.drs[:, 0:V], A.max), ["a0_0", "a0_1", "drs0"], ["x"])
+    op("p", lambda: t.matmul(T.ps[:, 0:V], T.b1[:], T.xe[:, 0:V], True, True), ["b1", "x"], ["ps"])
+    op("v", lambda: v.tensor_scalar(T.th0[:], T.thi[:], 16 * Z, None, A.add), ["thi"], ["th0"])
+    op("v", lambda: v.tensor_copy(T.thf[:], T.thi[:]), ["thi"], ["thf"])
+    choose(0, False)
+    send(0)
+    select(2)
+    if r > 0:
+        op("q", lambda: g.iota(T.base[:, 0:r, :], [[V, r], [0, 2]], 0, 0, allow_small_or_imprecise_dtypes=True), [], ["base0"])
+    if r < N - 1:
+        op("q", lambda: g.iota(T.base[:, r:N - 1, :], [[V, N - 1 - r], [0, 2]], V * (r + 1), 0, allow_small_or_imprecise_dtypes=True), [], ["base1"])
+    select(1)
+    select(0)
+    need("s", {"sent0": cnt["sent0"]})
+    dma("s", zu(10, 3), zu(0, 3), ["z0", "z1", "z2"], ["z10", "z11", "z12"], "dz1")
+    for u in (5, 6):
+        op("a", lambda: a.activation(zu(u), zu(0), F.Copy), ["z0"], ["z%d" % u])
+
+    op("v", lambda: v.tensor_copy(T.rc[:, :, 8], T.ci[:, 0, :]), ["ci"], ["rc0_7", "rc1_7"])
+    for hf in range(2):
+        lo, hi = hf * HV, hf * HV + HV
+        for q in range(7):
+            op("v", lambda: v.tensor_copy(T.rc[:, lo:hi, 1 + q], T.ci[:, 7 - q, lo:hi]), ["ci"], ["rc%d_%d" % (hf, q)])
+    op("p", lambda: t.matmul(T.pt[:, 0:V], T.ns[:], T.rc[:, :, 8], True, True), ["ns", "rc0_7", "rc1_7"], ["pt"])
+    n = 0
+    for hf in range(2):
+        rk = ["rc0"] + ["rc%d_%d" % (hf, q) for q in range(8)]
+        for j in range(16):
+            c = 15 - j
+            pd, pk = T["pd%d" % (n % 3)], "pd%d" % (n % 3)
+            n += 1
+            for q in range(2):
+                lo = hf * HV + 64 * q
+                out = pd[:, 512 * q:512 * q + 512]
+                op("p", lambda: t.matmul(out, T.sel[:, 128 * c:128 * c + 128], T.rc[:, lo:lo + 64, 1:9], True, j > 0), ["sel%d" % (c // 4)] + rk, [pk])
+                if j == 0:
+                    op("p", lambda: t.matmul(out, T.ns[:], T.rc[:, lo:lo + 64, 0:8], False, True), ["ns"] + rk, [pk])
+            op("a", lambda: a.activation(T.d0[:, hf * HV * P + j:(hf + 1) * HV * P:16], pd[:], F.Copy), [pk], ["d0_%d_%d" % (hf, j)])
+    op("v", lambda: v.tensor_scalar(T.b2[:], T.b1[:], 2.0, None, A.mult), ["b1"], ["b2"])
+    op("v", lambda: v.tensor_scalar(T.bm[:], T.b1[:], -1.0, None, A.mult), ["b1"], ["bm"])
+    op("v", lambda: v.tensor_scalar(T.drs[:, V:3 * V], T.dri[:, V:3 * V], Z, None, A.add), ["dri1"], ["drs1"])
+    after(0)
+    op("v", lambda: v.memset(zu(13, 3), Z), [], ["z13", "z14", "z15"])
+    own(0)
+    others(0)
+    scan()
+    choose(1, False)
+    send(1)
+    after(1)
+    own(1)
+    others(1)
+    op("a", lambda: a.activation(T.l32[:], T.la[:], F.Identity, bias=-Z), ["la"], ["l32"])
+    scan()
+    choose(2, True)
+    op("a", lambda: a.activation(T.x32[:], T.xe[:, 0:V], F.Identity, bias=-Z), ["x"], ["x32"])
+    dma("s", T.yx[:], T.x32[:], ["x32"], [], "dyx")
+    op("v", lambda: v.tensor_copy(T.l32[:, 0:L].indirect(T.raw[:, 0:2]), T.v32[:]), ["raw", "v32"], ["l32"])
+    dma("s", T.yl[:], T.l32[:, 0:V], ["l32"], [], "dyl")
+    need("s", dict(cnt))

@@ -6,40 +6,41 @@ P = 128
 W = V * P
 Z = -255.0
 U = W // 16
-NO = (N - 1) * CAP
-HV = V // 2
+PIECES = ((0, 96), (96, 192), (192, 256))
+MP = 96
 L = V + CAP
+NA = 9
+NO = 8
+MSG = {"m0": (0, (1, 2, 3, 4, 5, 6, 7, 0)), "m1": (1, (1, 2, 3, 4, 5, 6, 7))}
 X, K, C, Q, B = 16511.5, 128.0 / 32769.0, 12582912.0, 32769.0, 16383.248046875
+F32, BF, I32, U16 = "float32", "bfloat16", "int32", "uint16"
 
-SCRATCH = {
-    "x0i": ("sbuf", [128, V], "int32"), "dri": ("sbuf", [128, RO * V], "int32"), "thi": ("sbuf", [128, 1], "int32"),
-    "thf": ("sbuf", [128, 1], "float32"), "th0": ("sbuf", [128, 1], "float32"), "drs": ("sbuf", [128, RO * V], "bfloat16"),
-    "fani": ("sbuf", [128, 2048], "int32"), "ci": ("sbuf", [128, 8, V], "int32"),
-    "rc": ("sbuf", [128, V, 9], "bfloat16"),
-    "sel": ("sbuf", [128, 2048], "bfloat16"), "ones": ("sbuf", [128, 512], "bfloat16"), "nones": ("sbuf", [128, 128], "bfloat16"),
-    "ns": ("sbuf", [128, 128], "bfloat16"), "bt": ("sbuf", [128, 128], "bfloat16"),
-    "b1": ("sbuf", [128, 128], "bfloat16"), "b2": ("sbuf", [128, 128], "bfloat16"), "bm": ("sbuf", [128, 128], "bfloat16"),
-    "d0": ("sbuf", [128, W], "bfloat16"), "d1": ("sbuf", [128, W], "bfloat16"), "so": ("sbuf", [128, HV * P], "bfloat16"),
-    "pi": ("sbuf", [128, 2], "int32"), "jc": ("sbuf", [128, 1], "float32"), "jb": ("sbuf", [128, 1], "float32"),
-    "c33": ("sbuf", [128, L], "bfloat16"), "xe": ("sbuf", [128, L], "bfloat16"), "la": ("sbuf", [128, L], "bfloat16"),
-    "a0": ("sbuf", [128, V], "bfloat16"), "mx": ("sbuf", [128, V], "bfloat16"),
-    "chg": ("sbuf", [128, L], "bfloat16"), "cum": ("sbuf", [128, L], "bfloat16"), "le": ("sbuf", [128, L], "bfloat16"),
-    "sg": ("sbuf", [128, L], "bfloat16"), "acc": ("sbuf", [128, 1], "float32"), "cnt": ("sbuf", [128, 2], "float32"),
-    "tt2": ("sbuf", [128, 2], "float32"), "raw": ("sbuf", [128, 2], "uint16"),
-    "sb0": ("sbuf", [128, CAP + 2], "bfloat16"), "sb1": ("sbuf", [128, CAP + 2], "bfloat16"),
-    "land0": ("sbuf", [128, N - 1, CAP + 2], "bfloat16"), "land1": ("sbuf", [128, N - 1, CAP + 2], "bfloat16"),
-    "base": ("sbuf", [128, N - 1, 2], "float32"), "idf": ("sbuf", [128, N - 1, 2], "float32"),
-    "ids": ("sbuf", [128, 2 * (N - 1)], "uint16"), "ido": ("sbuf", [128, 2], "uint16"),
-    "w": ("sbuf", [128, NO], "float32"), "h": ("sbuf", [128, NO], "float32"), "d": ("sbuf", [128, NO], "float32"),
-    "of": ("sbuf", [128, NO], "uint16"), "ex": ("sbuf", [128, NO * 16], "bfloat16"),
-    "wo": ("sbuf", [128, CAP], "float32"), "ho": ("sbuf", [128, CAP], "float32"), "dd": ("sbuf", [128, CAP], "float32"),
-    "ofo": ("sbuf", [128, CAP], "uint16"), "exo": ("sbuf", [128, CAP * 16], "bfloat16"),
-    "l32": ("sbuf", [128, L], "float32"), "x32": ("sbuf", [128, V], "float32"), "v32": ("sbuf", [128, CAP], "float32"),
-    "pd0": ("psum", [128, 1024], "float32"), "pd1": ("psum", [128, 1024], "float32"), "pd2": ("psum", [128, 1024], "float32"),
-    "ps": ("psum", [128, 512], "float32"), "pt": ("psum", [128, 512], "float32"),
-}
-DMAS = ["dx", "dd0", "dth", "dcost", "dfan", "dd1", "dz0", "dz1", "dyx", "dyl"]
-SEMAPHORES = ["v", "a", "p", "q", "arr0", "arr1", "sent0", "sent1"] + DMAS
+SCRATCH = {}
+for _n, _m, _t in (
+        ("x0i", V, I32), ("dri", RO * V, I32), ("thi", 1, I32), ("thf", 1, F32), ("th0", 1, F32), ("drs", RO * V, BF),
+        ("fani", 2048, I32), ("sel", 2048, BF), ("ones", 512, BF), ("nones", 128, BF), ("ns", 128, BF), ("bt", 128, BF),
+        ("b1", 128, BF), ("b2", 128, BF), ("bm", 128, BF), ("d0", W, BF), ("d1", W, BF), ("so", MP * P, BF),
+        ("pi", 2, I32), ("jc", 1, F32), ("jb", 1, F32), ("c33", L, BF), ("xe", L, BF), ("la", L, BF), ("a0", V, BF), ("mx", V, BF),
+        ("chg", L, BF), ("cum", L, BF), ("le", L, BF), ("sg", L, BF), ("acc", 1, F32), ("cnt", 2, F32), ("tt2", 2, F32), ("raw", 2, U16),
+        ("sb0", CAP + 2, BF), ("sb1", CAP + 2, BF), ("wo", CAP, F32), ("ho", CAP, F32), ("dd", CAP, F32), ("ido", 2, U16),
+        ("ofo", CAP, U16), ("exo", CAP * 16, BF), ("l32", L, F32), ("x32", V, F32), ("v32", CAP, F32)):
+    SCRATCH[_n] = ("sbuf", [128, _m], _t)
+SCRATCH["ci"] = ("sbuf", [128, 8, V], I32)
+SCRATCH["rc"] = ("sbuf", [128, V, 9], BF)
+for _n, _m in (("pd0", 1536), ("pd1", 1536), ("ps", 512), ("pt", 512)):
+    SCRATCH[_n] = ("psum", [128, _m], F32)
+for _n, (_k, _s) in MSG.items():
+    _m = len(_s)
+    SCRATCH["land" + _n] = ("sbuf", [128, _m, CAP + 2], BF)
+    for _b in ("base", "idf"):
+        SCRATCH[_b + _n] = ("sbuf", [128, _m, 2], F32)
+    SCRATCH["ids" + _n] = ("sbuf", [128, 2 * _m], U16)
+    for _b in ("w", "h", "d"):
+        SCRATCH[_b + _n] = ("sbuf", [128, _m * CAP], F32)
+    SCRATCH["of" + _n] = ("sbuf", [128, _m * CAP], U16)
+    SCRATCH["ex" + _n] = ("sbuf", [128, _m * CAP * 16], BF)
+DMAS = ["dx", "dd0", "dth", "dfan", "dd1", "down", "dyx", "dyl"] + ["dc%d" % q for q in range(8)] + ["dz%d" % u for u in range(16)]
+SEMAPHORES = ["v", "a", "p", "q"] + ["arr" + n for n in MSG] + ["sent" + n for n in MSG] + DMAS
 
 
 def rank_program(g, core, T, topo):
@@ -89,16 +90,23 @@ def rank_program(g, core, T, topo):
     def dma(e, out, in_, rd, wr, sem):
         op(e, lambda: eng[e].dma_start(out, in_), rd, wr, sem, 16)
 
+    def zdma(us):
+        for u in us:
+            dma("s", zu(u), zu(0), ["z0"], ["z%d" % u], "dz%d" % u)
+
+    def zact(us):
+        for u in us:
+            op("a", lambda: a.activation(zu(u), zu(0), F.Copy), ["z0"], ["z%d" % u])
+
     dma("s", T.x0i[:], T.x0[:], [], ["x0i"], "dx")
     dma("s", T.dri[:, 0:V], T.drv[:, 0:V], [], ["dri0"], "dd0")
     dma("s", T.thi[:], T.th[:], [], ["thi"], "dth")
-    for q in range(8):
-        dma("s", T.ci[:, q, :], T.cost[:, 16 * V * q:16 * V * (q + 1)], [], ["ci"], "dcost")
-    dma("s", T.fani[:], T.fan[:], [], ["fan"], "dfan")
+    for q in (0, 7, 6, 5, 4, 3, 2, 1):
+        dma("s", T.ci[:, q, :], T.cost[:, 16 * V * q:16 * V * (q + 1)], [], ["ci%d" % q], "dc%d" % q)
     dma("s", T.dri[:, V:3 * V], T.drv[:, V:3 * V], [], ["dri1"], "dd1")
+    dma("s", T.fani[:], T.fan[:], [], ["fan"], "dfan")
 
     op("v", lambda: v.memset(T.ones[:], 1.0), [], ["ones"])
-    op("v", lambda: v.memset(T.nones[:], -1.0), [], ["nones"])
     op("q", lambda: g.affine_select(T.bt[:], T.ones[:, 0:128], [[-16, 8], [0, 16]], A.is_ge, 0.0, 0, 1), ["ones"], ["bt"])
     op("q", lambda: g.affine_select(T.b1[:], T.bt[:], [[16, 8], [0, 16]], A.is_ge, 0.0, 15, -1), ["bt"], ["b1"])
     op("q", lambda: g.iota(T.pi[:, 0:1], [[0, 1]], 0, 1), [], ["pi0"])
@@ -110,163 +118,177 @@ def rank_program(g, core, T, topo):
         s = T.sel[:, 512 * k:512 * k + 128 * m]
         op("q", lambda: g.affine_select(s, s, [[-1, m], [-16, 8], [0, 16]], A.not_equal, -1.0, -4 * k - 1, 1), ["sel%d" % k], ["sel%d" % k])
 
+    op("v", lambda: v.memset(zu(0), Z), [], ["z0"])
+    op("v", lambda: v.memset(T.nones[:], -1.0), [], ["nones"])
     op("q", lambda: g.affine_select(T.ns[:], T.nones[:], [[-16, 8], [0, 16]], A.is_equal, 0.0, 0, 1), ["nones"], ["ns"])
     select(3)
-    op("v", lambda: v.memset(zu(0), Z), [], ["z0"])
-    op("v", lambda: v.memset(T.rc[:, :, 0], 1024.0), [], ["rc0"])
+    select(1)
     op("v", lambda: v.memset(T.c33[:], float(CAP + 1)), [], ["c33"])
     op("v", lambda: v.memset(T.xe[:, V:L], Z), [], ["xp"])
-    op("v", lambda: v.memset(T.la[:], Z), [], ["la"])
     op("v", lambda: v.tensor_scalar(T.pi[:, 1:2], T.pi[:, 0:1], 15, None, A.bitwise_and), ["pi0"], ["pi1"])
     op("v", lambda: v.tensor_scalar(T.jc[:], T.pi[:, 1:2], 16.0, None, A.add), ["pi1"], ["jc"])
     op("v", lambda: v.tensor_scalar(T.jb[:], T.pi[:, 1:2], 0.5, None, A.add), ["pi1"], ["jb"])
-    op("v", lambda: v.memset(zu(1, 2), Z), [], ["z1", "z2"])
-    for u in (3, 4):
-        op("a", lambda: a.activation(zu(u), zu(0), F.Copy), ["z0"], ["z%d" % u])
-    dma("s", zu(7, 3), zu(0, 3), ["z0", "z1", "z2"], ["z7", "z8", "z9"], "dz0")
+    op("v", lambda: v.memset(T.rc[:, :, 0], 1024.0), [], ["rc0"])
+    op("v", lambda: v.memset(T.la[:], Z), [], ["la"])
+    zact((1, 2))
+    zdma((5, 6, 7))
 
     def choose(k, last):
-        th = T.th0 if k == 0 else T.thf
-        op("v", lambda: v.tensor_scalar(T.chg[:, 0:V], T.ps[:, 0:V], th[:, 0:1], None, A.is_ge), ["ps", "thf", "th0"], ["chg"])
-        op("v", lambda: v.tensor_scalar(T.chg[:, V:L], T.ps[:, 0:CAP], th[:, 0:1], None, A.is_lt), ["ps", "thf", "th0"], ["chp"])
+        th, tk = (T.th0, "th0") if k == 0 else (T.thf, "thf")
+        op("v", lambda: v.tensor_scalar(T.chg[:, 0:V], T.ps[:, 0:V], th[:, 0:1], None, A.is_ge), ["ps", tk], ["chg"])
+        op("v", lambda: v.tensor_scalar(T.chg[:, V:L], T.ps[:, 0:CAP], th[:, 0:1], None, A.is_lt), ["ps", tk], ["chp"])
         op("v", lambda: v.tensor_tensor_scan(T.cum[:], T.chg[:], T.c33[:], 0.0, A.add, A.min), ["chg", "chp", "c33"], ["cum"])
         op("a", lambda: a.activation(T.sg[:], T.cum[:], F.Sign, bias=T.jb[:, 0:1], scale=-1.0, accum_out=T.acc[:]), ["cum", "jb"], ["sg", "acc"])
         op("v", lambda: v.tensor_scalar(T.le[:], T.cum[:], T.jc[:, 0:1], None, A.is_le), ["cum", "jc"], ["le"])
         op("v", lambda: v.tensor_reduce(T.cnt[:, 1:2], T.le[:], AxisListType.X, A.add), ["le"], ["cnt1"])
-        op("v", lambda: v.tensor_scalar(T.cnt[:, 0:1], T.acc[:], 0.5, L / 2.0, A.mult, A.add), ["acc"], ["cnt0"])
-        op("v", lambda: v.tensor_copy(T.raw[:], T.cnt[:]), ["cnt0", "cnt1"], ["raw"])
+        op("v", lambda: v.tensor_scalar(T.raw[:, 0:1], T.acc[:], 0.5, L / 2.0, A.mult, A.add), ["acc"], ["raw0"])
+        op("v", lambda: v.tensor_copy(T.raw[:, 1:2], T.cnt[:, 1:2]), ["cnt1"], ["raw1"])
         if last:
-            op("v", lambda: v.tensor_scalar(T.v32[:], T.xe[:, 0:L].indirect(T.raw[:, 0:2]), -Z, None, A.add), ["x", "xp", "raw"], ["v32"])
+            op("v", lambda: v.tensor_scalar(T.v32[:], T.xe[:, 0:L].indirect(T.raw[:, 0:2]), -Z, None, A.add), ["x", "xp", "raw0", "raw1"], ["v32"])
             return
         sb = T["sb%d" % k]
+        op("v", lambda: v.tensor_scalar(T.cnt[:, 0:1], T.acc[:], 0.5, L / 2.0, A.mult, A.add), ["acc"], ["cnt0"])
+        op("v", lambda: v.tensor_copy(sb[:, 0:CAP], T.xe[:, 0:L].indirect(T.raw[:, 0:2])), ["x", "xp", "raw0", "raw1"], ["sbv%d" % k])
         op("v", lambda: v.tensor_scalar(T.tt2[:], T.cnt[:], float(V), -float(V), A.is_ge, A.mult), ["cnt0", "cnt1"], ["tt2"])
-        op("v", lambda: v.tensor_copy(sb[:, 0:CAP], T.xe[:, 0:L].indirect(T.raw[:, 0:2])), ["x", "xp", "raw"], ["sbv%d" % k])
         op("v", lambda: v.tensor_tensor(sb[:, CAP:CAP + 2], T.cnt[:], T.tt2[:], A.add), ["cnt0", "cnt1", "tt2"], ["sbi%d" % k])
 
-    def send(k):
+    def send(name):
+        k, shifts = MSG[name]
         sb = T["sb%d" % k]
         need("q", {"v": max(lw["sbv%d" % k][1], lw["sbi%d" % k][1])})
-        ids, dsts = [], []
-        for s in range(1, N):
-            q = (r + s) % N
-            rid, pid, _ = topo.addr(T.cores[q])
+        ids, dsts, n = [], [], 0
+        for i, s in enumerate(shifts):
+            if s == 0:
+                continue
+            rid, pid, _ = topo.addr(T.cores[(r + s) % N])
             ids.append(DstId(rid=rid, pnc=pid))
-            dsts.append(T["land%d" % k][:, r if r < q else r - 1, :])
+            dsts.append(T["land" + name][:, i, :])
+            n += len(topo.engines(T.cores[(r - s) % N], core))
         peer = T.cores[(r + 1) % N]
-        g.remote_dma_fused([RemoteDMATransfer(dst_ids=ids, dma_engine_mask=topo.mask(core, peer), remote_sem=T.sem["arr%d" % k], srcs=[sb[:]], dsts=dsts)],
-                           local_sem=T.sem["sent%d" % k])
-        cnt["sent%d" % k] = len(topo.engines(core, peer))
-        n = 0
-        for q in range(N):
-            if q != r:
-                n += len(topo.engines(T.cores[q], core))
-        cnt["arr%d" % k] = n
-        lw["land%d" % k] = ("arr%d" % k, n)
+        g.remote_dma_fused([RemoteDMATransfer(dst_ids=ids, dma_engine_mask=topo.mask(core, peer), remote_sem=T.sem["arr" + name], srcs=[sb[:]], dsts=dsts)],
+                           local_sem=T.sem["sent" + name])
+        cnt["sent" + name] = len(topo.engines(core, peer))
+        cnt["arr" + name] = n
+        lw["land" + name] = ("arr" + name, n)
 
-    def columns(idk, idap, w, h, d, of, tag):
-        op("v", lambda: v.tensor_scalar(w[:], T.fani[:, 0:2048].indirect(idap), X, K, A.subtract, A.mult), ["fan", idk], ["w" + tag])
-        op("v", lambda: v.tensor_scalar(h[:], w[:], C, C, A.add, A.subtract), ["w" + tag], ["h" + tag])
-        op("v", lambda: v.tensor_tensor(d[:], w[:], h[:], A.subtract), ["w" + tag, "h" + tag], ["d" + tag])
-        op("v", lambda: v.tensor_scalar(of[:], d[:], Q, B, A.mult, A.add), ["d" + tag], ["of" + tag])
+    def scatter(n, idops, ids, w, h, d, of, copies, exk, e16, tag):
+        steps = idops + [
+            lambda: op("v", lambda: v.tensor_scalar(w[:], T.fani[:, 0:2048].indirect(ids[:, 0:n // 16]), X, K, A.subtract, A.mult), ["fan", "ids" + tag], ["w" + tag]),
+            lambda: op("v", lambda: v.tensor_scalar(h[:], w[:], C, C, A.add, A.subtract), ["w" + tag], ["h" + tag]),
+            lambda: op("v", lambda: v.tensor_tensor(d[:], w[:], h[:], A.subtract), ["w" + tag, "h" + tag], ["d" + tag]),
+            lambda: op("v", lambda: v.tensor_scalar(of[:], d[:], Q, B, A.mult, A.add), ["d" + tag], ["of" + tag])]
+        done = 0
+        for i, step in enumerate(steps):
+            step()
+            upto = len(copies) * (i + 1) // len(steps)
+            for c in copies[done:upto]:
+                c()
+            done = upto
+        op("v", lambda: v.tensor_copy(T.d1[:, 0:W].indirect(of[:, 0:n]), e16[:]), ["of" + tag] + exk, zk)
 
     def own(k):
-        sb = T["sb%d" % k]
-        op("v", lambda: v.tensor_scalar(T.ido[:], sb[:, CAP:CAP + 2], float(V * r), None, A.add), ["sbi%d" % k], ["ido"])
-        for i in range(16):
-            op("v", lambda: v.tensor_copy(T.exo[:, i::16], sb[:, 0:CAP]), ["sbv%d" % k], ["exo%d" % i])
-        columns("ido", T.ido[:, 0:2], T.wo, T.ho, T.dd, T.ofo, "o")
-        op("v", lambda: v.tensor_copy(T.d1[:, 0:W].indirect(T.ofo[:, 0:CAP]), T.exo[:]), ["ofo"] + ["exo%d" % i for i in range(16)], zk)
+        sb, sv = T["sb%d" % k], "sbv%d" % k
+        exk = ["exo%d" % i for i in range(16)]
+        for i in range(NO):
+            op("a", lambda: a.activation(T.exo[:, i::16], sb[:, 0:CAP], F.Copy), [sv], [exk[i]])
+        idops = [lambda: op("v", lambda: v.tensor_scalar(T.ido[:], sb[:, CAP:CAP + 2], float(V * r), None, A.add), ["sbi%d" % k], ["idso"])]
+        copies = [lambda i=i: op("v", lambda: v.tensor_copy(T.exo[:, i::16], sb[:, 0:CAP]), [sv], [exk[i]]) for i in range(NO, 16)]
+        scatter(CAP, idops, T.ido, T.wo, T.ho, T.dd, T.ofo, copies, exk, T.exo, "o")
 
-    def others(k):
-        ld, lk = T["land%d" % k], "land%d" % k
-        ex = ["ex%d" % i for i in range(16)]
-        if k == 1:
-            for i in range(16):
-                op("a", lambda: a.activation(T.ex[:, i::16], ld[:, :, 0:CAP], F.Copy), [lk], [ex[i]])
-        op("v", lambda: v.tensor_tensor(T.idf[:], ld[:, :, CAP:CAP + 2], T.base[:], A.add), [lk, "base0", "base1"], ["idf"])
-        op("v", lambda: v.tensor_copy(T.ids[:], T.idf[:]), ["idf"], ["ids"])
-        columns("ids", T.ids[:, 0:2 * (N - 1)], T.w, T.h, T.d, T.of, "n")
-        if k == 0:
-            for i in range(16):
-                op("v", lambda: v.tensor_copy(T.ex[:, i::16], ld[:, :, 0:CAP]), [lk], [ex[i]])
-        op("v", lambda: v.tensor_copy(T.d1[:, 0:W].indirect(T.of[:, 0:NO]), T.ex[:]), ["ofn"] + ex, zk)
+    def take(name):
+        k, shifts = MSG[name]
+        n = len(shifts) * CAP
+        ld, lk = T["land" + name], ["land" + name] + (["lown"] if 0 in shifts else [])
+        e16, ids, idf = T["ex" + name], T["ids" + name], T["idf" + name]
+        exk = ["ex%s_%d" % (name, i) for i in range(16)]
+        na = NA if k == 1 else 0
+        for i in range(na):
+            op("a", lambda: a.activation(e16[:, i::16], ld[:, :, 0:CAP], F.Copy), lk, [exk[i]])
+        idops = [
+            lambda: op("v", lambda: v.tensor_tensor(idf[:], ld[:, :, CAP:CAP + 2], T["base" + name][:], A.add), lk + ["base" + name], ["idf" + name]),
+            lambda: op("v", lambda: v.tensor_copy(ids[:], idf[:]), ["idf" + name], ["ids" + name])]
+        copies = [lambda i=i: op("v", lambda: v.tensor_copy(e16[:, i::16], ld[:, :, 0:CAP]), lk, [exk[i]]) for i in range(na, 16)]
+        scatter(n, idops, ids, T["w" + name], T["h" + name], T["d" + name], T["of" + name], copies, exk, e16, name)
+
+    def bases(name):
+        for i, s in enumerate(MSG[name][1]):
+            op("q", lambda: g.iota(T["base" + name][:, i, :], [[0, 2]], V * ((r - s) % N), 0, allow_small_or_imprecise_dtypes=True), [], ["base%s_%d" % (name, i)])
+        lw["base" + name] = ("q", cnt["q"])
 
     def scan():
-        for c in range(2):
-            lo, hi = c * HV, c * HV + HV
-            op("v", lambda: v.tensor_tensor_scan(T.so[:], T.d0[:, lo * P:hi * P], T.d1[:, lo * P:hi * P], 0.0, A.add, A.max),
-               zk + ["d0_%d_%d" % (c, j) for j in range(16)], ["so"])
-            op("v", lambda: v.tensor_tensor(T.a0[:, lo:hi], T.so[:, P - 1::P], T.pt[:, lo:hi], A.add), ["so", "pt"], ["a0_%d" % c])
+        for c, (lo, hi) in enumerate(PIECES):
+            m = (hi - lo) * P
+            op("v", lambda: v.tensor_tensor_scan(T.so[:, 0:m], T.d0[:, lo * P:hi * P], T.d1[:, lo * P:hi * P], 0.0, A.add, A.max),
+               zk + ["d0_%d_%d" % (c, j) for j in range(8)], ["so"])
+            op("v", lambda: v.tensor_tensor(T.a0[:, lo:hi], T.so[:, P - 1:m:P], T.pt[:, lo:hi], A.add), ["so", "pt"], ["a0_%d" % c])
             op("v", lambda: v.tensor_tensor(T.xe[:, lo:hi], T.a0[:, lo:hi], T.pt[:, V + lo:V + hi], A.max), ["a0_%d" % c, "mm"], ["x"])
         op("v", lambda: v.tensor_tensor(T.mx[:], T.xe[:, 0:V], T.la[:, 0:V], A.max), ["x", "la"], ["mx"])
         op("p", lambda: t.matmul(T.ps[:, 0:V], T.bm[:], T.la[:, 0:V], True, False), ["bm", "la"], ["ps"])
         op("p", lambda: t.matmul(T.ps[:, 0:V], T.bm[:], T.xe[:, 0:V], False, False), ["bm", "x"], ["ps"])
         op("p", lambda: t.matmul(T.ps[:, 0:V], T.b2[:], T.mx[:], False, True), ["b2", "mx"], ["ps"])
 
-    def after(k):
-        op("v", lambda: v.tensor_copy(T.la[:, 0:L].indirect(T.raw[:, 0:2]), T["sb%d" % k][:, 0:CAP]), ["raw", "sbv%d" % k], ["la"])
-        op("v", lambda: v.tensor_scalar(T.a0[:], T.xe[:, 0:V], float(DEC), None, A.subtract), ["x"], ["a0_0", "a0_1"])
-        op("v", lambda: v.tensor_tensor(T.pt[:, V:2 * V], T.a0[:], T.drs[:, (k + 1) * V:(k + 2) * V], A.max), ["a0_0", "a0_1", "drs1", "pt"], ["mm"])
-        op("v", lambda: v.tensor_copy(T.xe[:, V:L], T.la[:, 0:CAP]), ["la"], ["xp"])
+    a0k = ["a0_%d" % c for c in range(len(PIECES))]
 
-    op("v", lambda: v.tensor_scalar(T.a0[:], T.x0i[:], DEC - Z, None, A.subtract), ["x0i"], ["a0_0", "a0_1"])
+    def after(k):
+        lo, hi = (k + 1) * V, (k + 2) * V
+        op("v", lambda: v.tensor_copy(T.la[:, 0:L].indirect(T.raw[:, 0:2]), T["sb%d" % k][:, 0:CAP]), ["raw0", "raw1", "sbv%d" % k], ["la"])
+        op("v", lambda: v.tensor_scalar(T.drs[:, lo:hi], T.dri[:, lo:hi], Z, None, A.add), ["dri1"], ["drs%d" % (k + 1)])
+        op("v", lambda: v.tensor_scalar(T.a0[:], T.xe[:, 0:V], float(DEC), None, A.subtract), ["x"], a0k)
+        op("v", lambda: v.tensor_copy(T.xe[:, V:L], T.la[:, 0:CAP]), ["la"], ["xp"])
+        op("v", lambda: v.tensor_tensor(T.pt[:, V:2 * V], T.a0[:], T.drs[:, lo:hi], A.max), a0k + ["drs%d" % (k + 1), "pt"], ["mm"])
+
+    op("v", lambda: v.tensor_scalar(T.a0[:], T.x0i[:], DEC - Z, None, A.subtract), ["x0i"], a0k)
     op("v", lambda: v.tensor_scalar(T.drs[:, 0:V], T.dri[:, 0:V], Z, None, A.add), ["dri0"], ["drs0"])
-    op("v", lambda: v.tensor_tensor(T.xe[:, 0:V], T.a0[:], T.drs[:, 0:V], A.max), ["a0_0", "a0_1", "drs0"], ["x"])
+    op("v", lambda: v.tensor_tensor(T.xe[:, 0:V], T.a0[:], T.drs[:, 0:V], A.max), a0k + ["drs0"], ["x"])
     op("p", lambda: t.matmul(T.ps[:, 0:V], T.b1[:], T.xe[:, 0:V], True, True), ["b1", "x"], ["ps"])
     op("v", lambda: v.tensor_scalar(T.th0[:], T.thi[:], 16 * Z, None, A.add), ["thi"], ["th0"])
     op("v", lambda: v.tensor_copy(T.thf[:], T.thi[:]), ["thi"], ["thf"])
     choose(0, False)
-    send(0)
+    send("m0")
     select(2)
-    if r > 0:
-        op("q", lambda: g.iota(T.base[:, 0:r, :], [[V, r], [0, 2]], 0, 0, allow_small_or_imprecise_dtypes=True), [], ["base0"])
-    if r < N - 1:
-        op("q", lambda: g.iota(T.base[:, r:N - 1, :], [[V, N - 1 - r], [0, 2]], V * (r + 1), 0, allow_small_or_imprecise_dtypes=True), [], ["base1"])
-    select(1)
     select(0)
-    need("s", {"sent0": cnt["sent0"]})
-    dma("s", zu(10, 3), zu(0, 3), ["z0", "z1", "z2"], ["z10", "z11", "z12"], "dz1")
-    for u in (5, 6):
-        op("a", lambda: a.activation(zu(u), zu(0), F.Copy), ["z0"], ["z%d" % u])
+    for name in MSG:
+        bases(name)
+    dma("s", T.landm0[:, 7, :], T.sb0[:], ["sbv0", "sbi0"], ["lown"], "down")
+    need("s", {"sentm0": cnt["sentm0"]})
+    zdma((8, 9, 10))
+    zact((3, 4))
 
-    op("v", lambda: v.tensor_copy(T.rc[:, :, 8], T.ci[:, 0, :]), ["ci"], ["rc0_7", "rc1_7"])
-    for hf in range(2):
-        lo, hi = hf * HV, hf * HV + HV
+    op("v", lambda: v.tensor_copy(T.rc[:, :, 8], T.ci[:, 0, :]), ["ci0"], ["rc0_7", "rc1_7"])
+    for c, (lo, hi) in enumerate(((0, MP), (MP, V))):
         for q in range(7):
-            op("v", lambda: v.tensor_copy(T.rc[:, lo:hi, 1 + q], T.ci[:, 7 - q, lo:hi]), ["ci"], ["rc%d_%d" % (hf, q)])
+            op("v", lambda: v.tensor_copy(T.rc[:, lo:hi, 1 + q], T.ci[:, 7 - q, lo:hi]), ["ci%d" % (7 - q)], ["rc%d_%d" % (c, q)])
     op("p", lambda: t.matmul(T.pt[:, 0:V], T.ns[:], T.rc[:, :, 8], True, True), ["ns", "rc0_7", "rc1_7"], ["pt"])
     n = 0
-    for hf in range(2):
-        rk = ["rc0"] + ["rc%d_%d" % (hf, q) for q in range(8)]
-        for j in range(16):
-            c = 15 - j
-            pd, pk = T["pd%d" % (n % 3)], "pd%d" % (n % 3)
+    for c, (lo, hi) in enumerate(PIECES):
+        rk = ["rc0"] + ["rc%d_%d" % (min(c, 1), q) for q in range(8)]
+        for j in range(8):
+            pd, pk = T["pd%d" % (n % 2)], "pd%d" % (n % 2)
             n += 1
-            for q in range(2):
-                lo = hf * HV + 64 * q
-                out = pd[:, 512 * q:512 * q + 512]
-                op("p", lambda: t.matmul(out, T.sel[:, 128 * c:128 * c + 128], T.rc[:, lo:lo + 64, 1:9], True, j > 0), ["sel%d" % (c // 4)] + rk, [pk])
-                if j == 0:
-                    op("p", lambda: t.matmul(out, T.ns[:], T.rc[:, lo:lo + 64, 0:8], False, True), ["ns"] + rk, [pk])
-            op("a", lambda: a.activation(T.d0[:, hf * HV * P + j:(hf + 1) * HV * P:16], pd[:], F.Copy), [pk], ["d0_%d_%d" % (hf, j)])
-    op("v", lambda: v.tensor_scalar(T.b2[:], T.b1[:], 2.0, None, A.mult), ["b1"], ["b2"])
-    op("v", lambda: v.tensor_scalar(T.bm[:], T.b1[:], -1.0, None, A.mult), ["b1"], ["bm"])
-    op("v", lambda: v.tensor_scalar(T.drs[:, V:3 * V], T.dri[:, V:3 * V], Z, None, A.add), ["dri1"], ["drs1"])
+            for s in range(lo, hi, 32):
+                for u in range(2):
+                    b = 15 - j - 8 * u
+                    out = pd[:, 16 * (s - lo) + u:16 * (s - lo) + 512:2]
+                    op("p", lambda: t.matmul(out, T.sel[:, 128 * b:128 * b + 128], T.rc[:, s:s + 32, 1:9], True, b < 15), ["sel%d" % (b // 4)] + rk, [pk])
+                    if b == 15:
+                        op("p", lambda: t.matmul(out, T.ns[:], T.rc[:, s:s + 32, 0:8], False, True), ["ns"] + rk, [pk])
+            op("a", lambda: a.activation(T.d0[:, lo * P + j:hi * P:8], pd[:, 0:16 * (hi - lo)], F.Copy), [pk], ["d0_%d_%d" % (c, j)])
+    op("a", lambda: a.activation(T.b2[:], T.b1[:], F.Copy, scale=2.0), ["b1"], ["b2"])
+    op("a", lambda: a.activation(T.bm[:], T.b1[:], F.Copy, scale=-1.0), ["b1"], ["bm"])
     after(0)
-    op("v", lambda: v.memset(zu(13, 3), Z), [], ["z13", "z14", "z15"])
-    own(0)
-    others(0)
+    op("v", lambda: v.memset(zu(11, 5), Z), [], ["z%d" % u for u in range(11, 16)])
+    take("m0")
     scan()
     choose(1, False)
-    send(1)
+    send("m1")
     after(1)
     own(1)
-    others(1)
+    take("m1")
     op("a", lambda: a.activation(T.l32[:], T.la[:], F.Identity, bias=-Z), ["la"], ["l32"])
     scan()
     choose(2, True)
     op("a", lambda: a.activation(T.x32[:], T.xe[:, 0:V], F.Identity, bias=-Z), ["x"], ["x32"])
     dma("s", T.yx[:], T.x32[:], ["x32"], [], "dyx")
-    op("v", lambda: v.tensor_copy(T.l32[:, 0:L].indirect(T.raw[:, 0:2]), T.v32[:]), ["raw", "v32"], ["l32"])
+    op("v", lambda: v.tensor_copy(T.l32[:, 0:L].indirect(T.raw[:, 0:2]), T.v32[:]), ["raw0", "raw1", "v32"], ["l32"])
     dma("s", T.yl[:], T.l32[:, 0:V], ["l32"], [], "dyl")
     need("s", dict(cnt))

from concourse.bass import DstId, RemoteDMATransfer
from concourse.mybir import AluOpType as A, AxisListType, ActivationFunctionType as F

N, V, CAP, RO, DEC = 8, 256, 32, 3, 24
P = 128
W = V * P
Z = -255.0
U = W // 16
PIECES = ((0, 96), (96, 192), (192, 256))
MP = 96
L = V + CAP
NA = 9
NO = 8
MSG = {"m0": (0, (1, 2, 3, 4, 5, 6, 7, 0)), "m1": (1, (1, 2, 3, 4, 5, 6, 7))}
X, K, C, Q, B = 16511.5, 128.0 / 32769.0, 12582912.0, 32769.0, 16383.248046875
F32, BF, I32, U16 = "float32", "bfloat16", "int32", "uint16"

SCRATCH = {}
for _n, _m, _t in (
        ("x0i", V, I32), ("dri", RO * V, I32), ("thi", 1, I32), ("thf", 1, F32), ("th0", 1, F32), ("drs", RO * V, BF),
        ("fani", 2048, I32), ("sel", 2048, BF), ("ones", 512, BF), ("nones", 128, BF), ("ns", 128, BF), ("bt", 128, BF),
        ("b1", 128, BF), ("b2", 128, BF), ("bm", 128, BF), ("d0", W, BF), ("d1", W, BF), ("so", MP * P, BF),
        ("pi", 2, I32), ("jc", 1, F32), ("jb", 1, F32), ("c33", L, BF), ("xe", L, BF), ("la", L, BF), ("a0", V, BF), ("mx", V, BF),
        ("chg", L, BF), ("cum", L, BF), ("le", L, BF), ("sg", L, BF), ("acc", 1, F32), ("cnt", 2, F32), ("tt2", 2, F32), ("raw", 2, U16),
        ("sb0", CAP + 2, BF), ("sb1", CAP + 2, BF), ("wo", CAP, F32), ("ho", CAP, F32), ("dd", CAP, F32), ("ido", 2, U16),
        ("ofo", CAP, U16), ("exo", CAP * 16, BF), ("l32", L, F32), ("x32", V, F32), ("v32", CAP, F32)):
    SCRATCH[_n] = ("sbuf", [128, _m], _t)
SCRATCH["ci"] = ("sbuf", [128, 8, V], I32)
SCRATCH["rc"] = ("sbuf", [128, V, 9], BF)
for _n, _m in (("pd0", 1536), ("pd1", 1536), ("ps", 512), ("pt", 512)):
    SCRATCH[_n] = ("psum", [128, _m], F32)
for _n, (_k, _s) in MSG.items():
    _m = len(_s)
    SCRATCH["land" + _n] = ("sbuf", [128, _m, CAP + 2], BF)
    for _b in ("base", "idf"):
        SCRATCH[_b + _n] = ("sbuf", [128, _m, 2], F32)
    SCRATCH["ids" + _n] = ("sbuf", [128, 2 * _m], U16)
    for _b in ("w", "h", "d"):
        SCRATCH[_b + _n] = ("sbuf", [128, _m * CAP], F32)
    SCRATCH["of" + _n] = ("sbuf", [128, _m * CAP], U16)
    SCRATCH["ex" + _n] = ("sbuf", [128, _m * CAP * 16], BF)
DMAS = ["dx", "dd0", "dth", "dfan", "dd1", "down", "dyx", "dyl"] + ["dc%d" % q for q in range(8)] + ["dz%d" % u for u in range(16)]
SEMAPHORES = ["v", "a", "p", "q"] + ["arr" + n for n in MSG] + ["sent" + n for n in MSG] + DMAS


def rank_program(g, core, T, topo):
    r = T.rank_of(core)
    if r is None:
        return
    eng = {"v": g.vector, "a": g.scalar, "p": g.tensor, "q": g, "s": g.sync}
    cnt, lw, lr, seen = {}, {}, {}, {e: {} for e in eng}

    def need(e, deps):
        for s in sorted(deps):
            if seen[e].get(s, 0) < deps[s]:
                eng[e].wait_ge(T.sem[s], deps[s])
                seen[e][s] = deps[s]

    def op(e, fn, rd, wr, sem=None, inc=1):
        deps = {}
        own = e if sem is None else None
        for k in rd:
            if k in lw:
                s, c = lw[k]
                deps[s] = max(deps.get(s, 0), c)
        for k in wr:
            if k in lw and not (e == "p" and lw[k][0] == "p"):
                s, c = lw[k]
                deps[s] = max(deps.get(s, 0), c)
            for s, c in lr.get(k, {}).items():
                if s != own:
                    deps[s] = max(deps.get(s, 0), c)
        need(e, deps)
        ins = fn()
        s = sem or e
        cnt[s] = cnt.get(s, 0) + inc
        ins.then_inc(T.sem[s], inc)
        for k in rd:
            lr.setdefault(k, {})[s] = cnt[s]
        for k in wr:
            lw[k] = (s, cnt[s])
            lr[k] = {}

    v, a, t = g.vector, g.scalar, g.tensor
    zk = ["z%d" % u for u in range(16)]

    def zu(u, n=1):
        return T.d1[:, u * U:(u + n) * U]

    def dma(e, out, in_, rd, wr, sem):
        op(e, lambda: eng[e].dma_start(out, in_), rd, wr, sem, 16)

    def zdma(us):
        for u in us:
            dma("s", zu(u), zu(0), ["z0"], ["z%d" % u], "dz%d" % u)

    def zact(us):
        for u in us:
            op("a", lambda: a.activation(zu(u), zu(0), F.Copy), ["z0"], ["z%d" % u])

    dma("s", T.x0i[:], T.x0[:], [], ["x0i"], "dx")
    dma("s", T.dri[:, 0:V], T.drv[:, 0:V], [], ["dri0"], "dd0")
    dma("s", T.thi[:], T.th[:], [], ["thi"], "dth")
    for q in (0, 7, 6, 5, 4, 3, 2, 1):
        dma("s", T.ci[:, q, :], T.cost[:, 16 * V * q:16 * V * (q + 1)], [], ["ci%d" % q], "dc%d" % q)
    dma("s", T.dri[:, V:3 * V], T.drv[:, V:3 * V], [], ["dri1"], "dd1")
    dma("s", T.fani[:], T.fan[:], [], ["fan"], "dfan")

    op("v", lambda: v.memset(T.ones[:], 1.0), [], ["ones"])
    op("q", lambda: g.affine_select(T.bt[:], T.ones[:, 0:128], [[-16, 8], [0, 16]], A.is_ge, 0.0, 0, 1), ["ones"], ["bt"])
    op("q", lambda: g.affine_select(T.b1[:], T.bt[:], [[16, 8], [0, 16]], A.is_ge, 0.0, 15, -1), ["bt"], ["b1"])
    op("q", lambda: g.iota(T.pi[:, 0:1], [[0, 1]], 0, 1), [], ["pi0"])

    def select(k):
        op("q", lambda: g.affine_select(T.sel[:, 512 * k:512 * k + 512], T.ones[:], [[-1, 4], [-16, 8], [0, 16]], A.is_equal, 0.0, -4 * k, 1),
           ["ones"], ["sel%d" % k])
        m = 3 if k == 3 else 4
        s = T.sel[:, 512 * k:512 * k + 128 * m]
        op("q", lambda: g.affine_select(s, s, [[-1, m], [-16, 8], [0, 16]], A.not_equal, -1.0, -4 * k - 1, 1), ["sel%d" % k], ["sel%d" % k])

    op("v", lambda: v.memset(zu(0), Z), [], ["z0"])
    op("v", lambda: v.memset(T.nones[:], -1.0), [], ["nones"])
    op("q", lambda: g.affine_select(T.ns[:], T.nones[:], [[-16, 8], [0, 16]], A.is_equal, 0.0, 0, 1), ["nones"], ["ns"])
    select(3)
    select(1)
    op("v", lambda: v.memset(T.c33[:], float(CAP + 1)), [], ["c33"])
    op("v", lambda: v.memset(T.xe[:, V:L], Z), [], ["xp"])
    op("v", lambda: v.tensor_scalar(T.pi[:, 1:2], T.pi[:, 0:1], 15, None, A.bitwise_and), ["pi0"], ["pi1"])
    op("v", lambda: v.tensor_scalar(T.jc[:], T.pi[:, 1:2], 16.0, None, A.add), ["pi1"], ["jc"])
    op("v", lambda: v.tensor_scalar(T.jb[:], T.pi[:, 1:2], 0.5, None, A.add), ["pi1"], ["jb"])
    op("v", lambda: v.memset(T.rc[:, :, 0], 1024.0), [], ["rc0"])
    op("v", lambda: v.memset(T.la[:], Z), [], ["la"])
    zact((1, 2))
    zdma((5, 6, 7))

    def choose(k, last):
        th, tk = (T.th0, "th0") if k == 0 else (T.thf, "thf")
        op("v", lambda: v.tensor_scalar(T.chg[:, 0:V], T.ps[:, 0:V], th[:, 0:1], None, A.is_ge), ["ps", tk], ["chg"])
        op("v", lambda: v.tensor_scalar(T.chg[:, V:L], T.ps[:, 0:CAP], th[:, 0:1], None, A.is_lt), ["ps", tk], ["chp"])
        op("v", lambda: v.tensor_tensor_scan(T.cum[:], T.chg[:], T.c33[:], 0.0, A.add, A.min), ["chg", "chp", "c33"], ["cum"])
        op("a", lambda: a.activation(T.sg[:], T.cum[:], F.Sign, bias=T.jb[:, 0:1], scale=-1.0, accum_out=T.acc[:]), ["cum", "jb"], ["sg", "acc"])
        op("v", lambda: v.tensor_scalar(T.le[:], T.cum[:], T.jc[:, 0:1], None, A.is_le), ["cum", "jc"], ["le"])
        op("v", lambda: v.tensor_reduce(T.cnt[:, 1:2], T.le[:], AxisListType.X, A.add), ["le"], ["cnt1"])
        op("v", lambda: v.tensor_scalar(T.raw[:, 0:1], T.acc[:], 0.5, L / 2.0, A.mult, A.add), ["acc"], ["raw0"])
        op("v", lambda: v.tensor_copy(T.raw[:, 1:2], T.cnt[:, 1:2]), ["cnt1"], ["raw1"])
        if last:
            op("v", lambda: v.tensor_scalar(T.v32[:], T.xe[:, 0:L].indirect(T.raw[:, 0:2]), -Z, None, A.add), ["x", "xp", "raw0", "raw1"], ["v32"])
            return
        sb = T["sb%d" % k]
        op("v", lambda: v.tensor_scalar(T.cnt[:, 0:1], T.acc[:], 0.5, L / 2.0, A.mult, A.add), ["acc"], ["cnt0"])
        op("v", lambda: v.tensor_copy(sb[:, 0:CAP], T.xe[:, 0:L].indirect(T.raw[:, 0:2])), ["x", "xp", "raw0", "raw1"], ["sbv%d" % k])
        op("v", lambda: v.tensor_scalar(T.tt2[:], T.cnt[:], float(V), -float(V), A.is_ge, A.mult), ["cnt0", "cnt1"], ["tt2"])
        op("v", lambda: v.tensor_tensor(sb[:, CAP:CAP + 2], T.cnt[:], T.tt2[:], A.add), ["cnt0", "cnt1", "tt2"], ["sbi%d" % k])

    def send(name):
        k, shifts = MSG[name]
        sb = T["sb%d" % k]
        need("q", {"v": max(lw["sbv%d" % k][1], lw["sbi%d" % k][1])})
        ids, dsts, n = [], [], 0
        for i, s in enumerate(shifts):
            if s == 0:
                continue
            rid, pid, _ = topo.addr(T.cores[(r + s) % N])
            ids.append(DstId(rid=rid, pnc=pid))
            dsts.append(T["land" + name][:, i, :])
            n += len(topo.engines(T.cores[(r - s) % N], core))
        peer = T.cores[(r + 1) % N]
        g.remote_dma_fused([RemoteDMATransfer(dst_ids=ids, dma_engine_mask=topo.mask(core, peer), remote_sem=T.sem["arr" + name], srcs=[sb[:]], dsts=dsts)],
                           local_sem=T.sem["sent" + name])
        cnt["sent" + name] = len(topo.engines(core, peer))
        cnt["arr" + name] = n
        lw["land" + name] = ("arr" + name, n)

    def scatter(n, idops, ids, w, h, d, of, copies, exk, e16, tag):
        steps = idops + [
            lambda: op("v", lambda: v.tensor_scalar(w[:], T.fani[:, 0:2048].indirect(ids[:, 0:n // 16]), X, K, A.subtract, A.mult), ["fan", "ids" + tag], ["w" + tag]),
            lambda: op("v", lambda: v.tensor_scalar(h[:], w[:], C, C, A.add, A.subtract), ["w" + tag], ["h" + tag]),
            lambda: op("v", lambda: v.tensor_tensor(d[:], w[:], h[:], A.subtract), ["w" + tag, "h" + tag], ["d" + tag]),
            lambda: op("v", lambda: v.tensor_scalar(of[:], d[:], Q, B, A.mult, A.add), ["d" + tag], ["of" + tag])]
        done = 0
        for i, step in enumerate(steps):
            step()
            upto = len(copies) * (i + 1) // len(steps)
            for c in copies[done:upto]:
                c()
            done = upto
        op("v", lambda: v.tensor_copy(T.d1[:, 0:W].indirect(of[:, 0:n]), e16[:]), ["of" + tag] + exk, zk)

    def own(k):
        sb, sv = T["sb%d" % k], "sbv%d" % k
        exk = ["exo%d" % i for i in range(16)]
        for i in range(NO):
            op("a", lambda: a.activation(T.exo[:, i::16], sb[:, 0:CAP], F.Copy), [sv], [exk[i]])
        idops = [lambda: op("v", lambda: v.tensor_scalar(T.ido[:], sb[:, CAP:CAP + 2], float(V * r), None, A.add), ["sbi%d" % k], ["idso"])]
        copies = [lambda i=i: op("v", lambda: v.tensor_copy(T.exo[:, i::16], sb[:, 0:CAP]), [sv], [exk[i]]) for i in range(NO, 16)]
        scatter(CAP, idops, T.ido, T.wo, T.ho, T.dd, T.ofo, copies, exk, T.exo, "o")

    def take(name):
        k, shifts = MSG[name]
        n = len(shifts) * CAP
        ld, lk = T["land" + name], ["land" + name] + (["lown"] if 0 in shifts else [])
        e16, ids, idf = T["ex" + name], T["ids" + name], T["idf" + name]
        exk = ["ex%s_%d" % (name, i) for i in range(16)]
        na = NA if k == 1 else 0
        for i in range(na):
            op("a", lambda: a.activation(e16[:, i::16], ld[:, :, 0:CAP], F.Copy), lk, [exk[i]])
        idops = [
            lambda: op("v", lambda: v.tensor_tensor(idf[:], ld[:, :, CAP:CAP + 2], T["base" + name][:], A.add), lk + ["base" + name], ["idf" + name]),
            lambda: op("v", lambda: v.tensor_copy(ids[:], idf[:]), ["idf" + name], ["ids" + name])]
        copies = [lambda i=i: op("v", lambda: v.tensor_copy(e16[:, i::16], ld[:, :, 0:CAP]), lk, [exk[i]]) for i in range(na, 16)]
        scatter(n, idops, ids, T["w" + name], T["h" + name], T["d" + name], T["of" + name], copies, exk, e16, name)

    def bases(name):
        for i, s in enumerate(MSG[name][1]):
            op("q", lambda: g.iota(T["base" + name][:, i, :], [[0, 2]], V * ((r - s) % N), 0, allow_small_or_imprecise_dtypes=True), [], ["base%s_%d" % (name, i)])
        lw["base" + name] = ("q", cnt["q"])

    def scan():
        for c, (lo, hi) in enumerate(PIECES):
            m = (hi - lo) * P
            op("v", lambda: v.tensor_tensor_scan(T.so[:, 0:m], T.d0[:, lo * P:hi * P], T.d1[:, lo * P:hi * P], 0.0, A.add, A.max),
               zk + ["d0_%d_%d" % (c, j) for j in range(8)], ["so"])
            op("v", lambda: v.tensor_tensor(T.a0[:, lo:hi], T.so[:, P - 1:m:P], T.pt[:, lo:hi], A.add), ["so", "pt"], ["a0_%d" % c])
            op("v", lambda: v.tensor_tensor(T.xe[:, lo:hi], T.a0[:, lo:hi], T.pt[:, V + lo:V + hi], A.max), ["a0_%d" % c, "mm"], ["x"])
        op("v", lambda: v.tensor_tensor(T.mx[:], T.xe[:, 0:V], T.la[:, 0:V], A.max), ["x", "la"], ["mx"])
        op("p", lambda: t.matmul(T.ps[:, 0:V], T.bm[:], T.la[:, 0:V], True, False), ["bm", "la"], ["ps"])
        op("p", lambda: t.matmul(T.ps[:, 0:V], T.bm[:], T.xe[:, 0:V], False, False), ["bm", "x"], ["ps"])
        op("p", lambda: t.matmul(T.ps[:, 0:V], T.b2[:], T.mx[:], False, True), ["b2", "mx"], ["ps"])

    a0k = ["a0_%d" % c for c in range(len(PIECES))]

    def after(k):
        lo, hi = (k + 1) * V, (k + 2) * V
        op("v", lambda: v.tensor_copy(T.la[:, 0:L].indirect(T.raw[:, 0:2]), T["sb%d" % k][:, 0:CAP]), ["raw0", "raw1", "sbv%d" % k], ["la"])
        op("v", lambda: v.tensor_scalar(T.drs[:, lo:hi], T.dri[:, lo:hi], Z, None, A.add), ["dri1"], ["drs%d" % (k + 1)])
        op("v", lambda: v.tensor_scalar(T.a0[:], T.xe[:, 0:V], float(DEC), None, A.subtract), ["x"], a0k)
        op("v", lambda: v.tensor_copy(T.xe[:, V:L], T.la[:, 0:CAP]), ["la"], ["xp"])
        op("v", lambda: v.tensor_tensor(T.pt[:, V:2 * V], T.a0[:], T.drs[:, lo:hi], A.max), a0k + ["drs%d" % (k + 1), "pt"], ["mm"])

    op("v", lambda: v.tensor_scalar(T.a0[:], T.x0i[:], DEC - Z, None, A.subtract), ["x0i"], a0k)
    op("v", lambda: v.tensor_scalar(T.drs[:, 0:V], T.dri[:, 0:V], Z, None, A.add), ["dri0"], ["drs0"])
    op("v", lambda: v.tensor_tensor(T.xe[:, 0:V], T.a0[:], T.drs[:, 0:V], A.max), a0k + ["drs0"], ["x"])
    op("p", lambda: t.matmul(T.ps[:, 0:V], T.b1[:], T.xe[:, 0:V], True, True), ["b1", "x"], ["ps"])
    op("v", lambda: v.tensor_scalar(T.th0[:], T.thi[:], 16 * Z, None, A.add), ["thi"], ["th0"])
    op("v", lambda: v.tensor_copy(T.thf[:], T.thi[:]), ["thi"], ["thf"])
    choose(0, False)
    send("m0")
    select(2)
    select(0)
    for name in MSG:
        bases(name)
    dma("s", T.landm0[:, 7, :], T.sb0[:], ["sbv0", "sbi0"], ["lown"], "down")
    need("s", {"sentm0": cnt["sentm0"]})
    zdma((8, 9, 10))
    zact((3, 4))

    op("v", lambda: v.tensor_copy(T.rc[:, :, 8], T.ci[:, 0, :]), ["ci0"], ["rc0_7", "rc1_7"])
    for c, (lo, hi) in enumerate(((0, MP), (MP, V))):
        for q in range(7):
            op("v", lambda: v.tensor_copy(T.rc[:, lo:hi, 1 + q], T.ci[:, 7 - q, lo:hi]), ["ci%d" % (7 - q)], ["rc%d_%d" % (c, q)])
    op("p", lambda: t.matmul(T.pt[:, 0:V], T.ns[:], T.rc[:, :, 8], True, True), ["ns", "rc0_7", "rc1_7"], ["pt"])
    n = 0
    for c, (lo, hi) in enumerate(PIECES):
        rk = ["rc0"] + ["rc%d_%d" % (min(c, 1), q) for q in range(8)]
        for j in range(8):
            pd, pk = T["pd%d" % (n % 2)], "pd%d" % (n % 2)
            n += 1
            for s in range(lo, hi, 32):
                for u in range(2):
                    b = 15 - j - 8 * u
                    out = pd[:, 16 * (s - lo) + u:16 * (s - lo) + 512:2]
                    op("p", lambda: t.matmul(out, T.sel[:, 128 * b:128 * b + 128], T.rc[:, s:s + 32, 1:9], True, b < 15), ["sel%d" % (b // 4)] + rk, [pk])
                    if b == 15:
                        op("p", lambda: t.matmul(out, T.ns[:], T.rc[:, s:s + 32, 0:8], False, True), ["ns"] + rk, [pk])
            op("a", lambda: a.activation(T.d0[:, lo * P + j:hi * P:8], pd[:, 0:16 * (hi - lo)], F.Copy), [pk], ["d0_%d_%d" % (c, j)])
    op("a", lambda: a.activation(T.b2[:], T.b1[:], F.Copy, scale=2.0), ["b1"], ["b2"])
    op("a", lambda: a.activation(T.bm[:], T.b1[:], F.Copy, scale=-1.0), ["b1"], ["bm"])
    after(0)
    op("v", lambda: v.memset(zu(11, 5), Z), [], ["z%d" % u for u in range(11, 16)])
    take("m0")
    scan()
    choose(1, False)
    send("m1")
    after(1)
    own(1)
    take("m1")
    op("a", lambda: a.activation(T.l32[:], T.la[:], F.Identity, bias=-Z), ["la"], ["l32"])
    scan()
    choose(2, True)
    op("a", lambda: a.activation(T.x32[:], T.xe[:, 0:V], F.Identity, bias=-Z), ["x"], ["x32"])
    dma("s", T.yx[:], T.x32[:], ["x32"], [], "dyx")
    op("v", lambda: v.tensor_copy(T.l32[:, 0:L].indirect(T.raw[:, 0:2]), T.v32[:]), ["raw0", "raw1", "v32"], ["l32"])
    dma("s", T.yl[:], T.l32[:, 0:V], ["l32"], [], "dyl")
    need("s", dict(cnt))
